import numpy as np
import ml_dtypes


def mxq(x, axis, fmt="e4m3"):
    dtype, down = {"e4m3": (ml_dtypes.float8_e4m3fn, 7), "e5m2": (ml_dtypes.float8_e5m2, 14)}[fmt]
    v = np.moveaxis(np.asarray(x, np.float32).astype(ml_dtypes.bfloat16).astype(np.float64), axis, -1)
    blocks = v.reshape(v.shape[:-1] + (-1, 32))
    amax = np.abs(blocks).max(-1, keepdims=True)
    byte = np.maximum(np.where(amax > 0, np.frexp(amax)[1] - 1 + 127, 0) - down, 1)
    scale = np.exp2(byte - 127.0)
    codes = (blocks / scale).astype(np.float32).astype(dtype).astype(np.float64)
    return np.moveaxis((codes * scale).reshape(v.shape), -1, axis)


WIDE = False


def mx_kscale(k):
    if not WIDE:
        return np.ones(k)
    levels = np.array([18, -18])
    if k % 512:
        return np.exp2(np.random.permutation(np.resize(levels, k // 32))).repeat(32)
    a = np.empty((k // 512, 16))
    for p in range(k // 512):
        a[p, :8] = np.random.permutation(np.resize(levels, 8))
        for g in range(8):
            far = levels[np.abs(levels - a[p, g]) >= 10]
            a[p, g + 8] = far[np.random.randint(len(far))]
    return np.exp2(a.ravel()).repeat(32)


def f64(x):
    return np.asarray(x).astype(np.float64)


def striped(idx):
    return np.tile(np.asarray(idx).reshape(-1, 16).T, (8, 1)).astype(np.uint16)


def unstriped(offs):
    return offs[:16].T.reshape(-1).astype(np.int64)


B, N, T, D, R, TU = 1, 512, 2048, 512, 512, 2048


def setup_inputs():
    n = np.random.standard_normal
    idx = np.random.permutation(T)[:B * N]
    uidx = np.random.permutation(TU)[:B * R]
    s = mx_kscale(D)[:, None]
    z = np.ones(TU)
    z[uidx] = mx_kscale(B * R)
    u = np.ones(T)
    u[idx] = mx_kscale(B * N)
    r = np.random.uniform(0.5, 2.0, T) * u
    ur = np.random.uniform(0.5, 2.0, TU) * z
    return {
        "uT": (n((D, TU)) * s / ur).astype(np.float32),
        "vT": (n((D, T)) * (1.00 / np.sqrt(D)) / s / r).astype(np.float32),
        "y": np.random.randint(0, 2, (B, R, N)).astype(np.float32),
        "us": ur[uidx].reshape(B, R, 1).astype(np.float32),
        "ts": np.tile(r, (128, 1)).astype(np.float32),
        "kb": np.tile(0.5 * n(T), (128, 1)).astype(np.float32),
        "offs": striped(idx),
        "uoffs": striped(uidx),
    }


def reference(uT, vT, y, us, ts, kb, offs, uoffs):
    idx = unstriped(offs)
    pick = lambda x: x[:, idx].reshape(x.shape[0], B, N).transpose(1, 0, 2)
    uidx = unstriped(uoffs)
    w = pick(f64(vT))
    x = f64(uT)[:, uidx].reshape(D, B, R).transpose(1, 0, 2)
    a = mxq(x, 1, "e4m3").transpose(0, 2, 1) @ mxq(w, 1, "e4m3")
    sc = f64(us) * pick(f64(ts))[:, :1, :]
    a = a * sc
    a = a + pick(f64(kb))[:, :1, :]
    g = (1.0 / (1.0 + np.exp(-a)) - f64(y))
    h = sc * g
    dv = mxq(x, 2, "e4m3") @ mxq(h, 1, "e5m2")
    gv = np.zeros((D, T))
    gv[:, idx] = dv.transpose(1, 0, 2).reshape(D, B * N)
    du = mxq(w, 2, "e4m3") @ mxq(h, 2, "e5m2").transpose(0, 2, 1)
    gu = np.zeros((D, TU))
    gu[:, uidx] = du.transpose(1, 0, 2).reshape(D, B * R)
    return gv, gu

@@ -1,0 +1,255 @@
+from contextlib import ExitStack
+
+import concourse.mybir as mybir
+from concourse.masks import make_identity
+
+F32 = mybir.dt.float32
+BF16 = mybir.dt.bfloat16
+U32 = mybir.dt.uint32
+U16 = mybir.dt.uint16
+U8 = mybir.dt.uint8
+E4M3 = mybir.dt.float8_e4m3fn_x4
+E5M2 = mybir.dt.float8_e5m2_x4
+MULT = mybir.AluOpType.mult
+SUB = mybir.AluOpType.subtract
+SIGMOID = mybir.ActivationFunctionType.Sigmoid
+
+P = 128
+PACK = 4
+K = P * PACK
+TABLE = 2048
+FLOPS = 3 * 2 * K * K * K
+
+
+def tile_attend_gmf_nce_vu_kb_kernel(tc, uT, vT, y, us, ts, kb, offs, uoffs, out_0, out_1):
+    nc = tc.nc
+    with ExitStack() as ctx:
+        sb = ctx.enter_context(tc.tile_pool(name="sb", bufs=1))
+        ps = ctx.enter_context(tc.psum_pool(name="ps", bufs=1))
+
+        def tile(name, cols, dtype):
+            return sb.tile([P, cols], dtype, name=name, align_bytes=64)
+
+        banks = [ps.tile([P, K], F32, name="bank%d" % b) for b in range(8)]
+
+        tail_list = tile("tail_list", K // 16, U16)
+        head_list = tile("head_list", K // 16, U16)
+        u_planes = [tile("u_plane%d" % t, TABLE, F32) for t in range(PACK)]
+        v_planes = [tile("v_plane%d" % t, TABLE, F32) for t in range(PACK)]
+        labels = tile("labels", PACK * K, F32)
+        us4 = tile("us4", PACK, F32)
+        ts_row = tile("ts_row", TABLE, F32)
+        kb_row = tile("kb_row", TABLE, F32)
+
+        u_rows = uT.rearrange("(p t) n -> p t n", t=PACK)
+        v_rows = vT.rearrange("(p t) n -> p t n", t=PACK)
+        nc.sync.dma_start(out=u_planes[0][:], in_=u_rows[:, 0, :])
+        nc.sync.dma_start(head_list[:], uoffs)
+        nc.sync.dma_start(tail_list[:], offs)
+        nc.scalar.dma_start(out=ts_row[P - 1 : P, :], in_=ts[0:1, :])
+        nc.scalar.dma_start(out=kb_row[P - 1 : P, :], in_=kb[0:1, :])
+        nc.scalar.dma_start(out=us4[:], in_=us[0].rearrange("(s t) o -> s (t o)", t=PACK))
+        nc.vector.memset(ts_row[0 : P - 1, :], 0.0)
+        nc.vector.memset(kb_row[0 : P - 1, :], 0.0)
+        for t in range(1, PACK):
+            nc.sync.dma_start(out=u_planes[t][:], in_=u_rows[:, t, :])
+        for t in range(PACK):
+            nc.sync.dma_start(out=v_planes[t][:], in_=v_rows[:, t, :])
+        nc.sync.dma_start(out=labels[:], in_=y[0].rearrange("(s t) i -> s (t i)", t=PACK))
+
+        ident = tile("ident", P, F32)
+        make_identity(nc, ident[:])
+        warm = tile("warm", 1, F32)
+        nc.scalar.activation(out=warm[:], in_=ident[:, 0:1], func=SIGMOID)
+        tail_windows = [tile("tail_window%d" % w, TABLE, F32) for w in range(2)]
+        head_windows = [tile("head_window%d" % w, TABLE, F32) for w in range(2)]
+        for window in tail_windows + head_windows:
+            nc.gpsimd.memset(window[:], 0.0)
+
+        def turn(bank, block, src):
+            nc.tensor.transpose(bank[:, block * P : (block + 1) * P], src, ident[:])
+
+        def quantize(name, src, fmt, pieces):
+            codes = tile(name + "_codes", K, U32)
+            scales = tile(name + "_scales", K, U8)
+            width = K // pieces
+
+            def piece(n):
+                cols = slice(n * width, (n + 1) * width)
+                nc.vector.quantize_mx(
+                    out=codes[:, cols].bitcast(fmt),
+                    scales=scales[:, cols],
+                    in_=src[:, PACK * n * width : PACK * (n + 1) * width],
+                )
+
+            return codes, scales, piece
+
+        def product(bank, stat, block, stat_fmt, mov, mov_fmt):
+            cols = slice(block * P, (block + 1) * P)
+            nc.tensor.matmul_mx(
+                out=bank[:],
+                lhsT=stat[0][:, cols].bitcast(stat_fmt),
+                lhsT_scale=stat[1][:, cols],
+                rhs=mov[0][:].bitcast(mov_fmt),
+                rhs_scale=mov[1][:],
+                start=True,
+                stop=True,
+            )
+
+        def gather_plane(picked, t, plane, offsets):
+            nc.vector.tensor_copy(picked[:, t * K : (t + 1) * K], plane[:].indirect(offsets[:]))
+
+        def turn_plane(picked, t, bank, turned):
+            words = picked[:].bitcast(F32)
+            for u in range(2):
+                turn(bank, u, words[:, 256 * t + u : 256 * (t + 1) : 2])
+            nc.scalar.copy(
+                out=turned[:].bitcast(F32)[:, 256 * t : 256 * (t + 1)].rearrange("s (p u) -> s p u", u=2),
+                in_=bank[:, 0:256].rearrange("s (u p) -> s p u", u=2),
+            )
+
+        x_picked = tile("x_picked", PACK * K, BF16)
+        x_turned = tile("x_turned", PACK * K, BF16)
+        gather_plane(x_picked, 0, u_planes[0], head_list)
+        turn_plane(x_picked, 0, banks[4], x_turned)
+
+        us_free = tile("us_free", K, F32)
+        for t in range(PACK):
+            turn(banks[3], t, us4[:, t : t + 1].to_broadcast([P, P]))
+        nc.scalar.copy(out=us_free[:], in_=banks[3][:])
+
+        gather_plane(x_picked, 1, u_planes[1], head_list)
+        turn_plane(x_picked, 1, banks[5], x_turned)
+
+        ts_picked = tile("ts_picked", K, F32)
+        kb_picked = tile("kb_picked", K, F32)
+        ts_cols = tile("ts_cols", PACK, F32)
+        kb_cols = tile("kb_cols", PACK, F32)
+        for row, picked, cols, bank in ((ts_row, ts_picked, ts_cols, banks[0]), (kb_row, kb_picked, kb_cols, banks[1])):
+            nc.vector.tensor_copy(picked[:], row[:].indirect(tail_list[:]))
+            for j in range(PACK):
+                turn(bank, j, picked[:, j * P : (j + 1) * P])
+            nc.scalar.copy(out=cols[:], in_=bank[:, P - 1 : K : P])
+        for j in range(PACK):
+            turn(banks[2], j, ts_cols[:, j : j + 1].to_broadcast([P, P]))
+
+        for t in range(2, PACK):
+            gather_plane(x_picked, t, u_planes[t], head_list)
+            turn_plane(x_picked, t, banks[4 + t], x_turned)
+
+        both_scales = tile("both_scales", PACK * K, F32)
+        nc.vector.tensor_tensor(
+            both_scales[:].rearrange("s (c t) -> s c t", t=PACK),
+            banks[2][:].unsqueeze(2).to_broadcast([P, K, PACK]),
+            us4[:].unsqueeze(1).to_broadcast([P, K, PACK]),
+            MULT,
+        )
+
+        x_woven = tile("x_woven", PACK * K, BF16)
+        nc.scalar.copy(
+            out=x_woven[:].rearrange("p (a s t) -> p s a t", a=PACK, t=PACK),
+            in_=x_picked[:].rearrange("p (t s a) -> p s a t", a=PACK, t=PACK),
+        )
+
+        w_picked = tile("w_picked", PACK * K, BF16)
+        w_turned = tile("w_turned", PACK * K, BF16)
+        gather_plane(w_picked, 0, v_planes[0], tail_list)
+        turn_plane(w_picked, 0, banks[0], w_turned)
+        x_by_row = quantize("x_by_row", x_turned, E4M3, 1)
+        x_by_row[2](0)
+        gather_plane(w_picked, 1, v_planes[1], tail_list)
+        turn_plane(w_picked, 1, banks[1], w_turned)
+        x_by_feature = quantize("x_by_feature", x_woven, E4M3, 1)
+        x_by_feature[2](0)
+        for t in range(2, PACK):
+            gather_plane(w_picked, t, v_planes[t], tail_list)
+            turn_plane(w_picked, t, banks[t], w_turned)
+
+        w_woven = tile("w_woven", PACK * K, BF16)
+        woven_view = w_woven[:].rearrange("p (g i t) -> p g t i", i=PACK, t=PACK)
+        picked_view = w_picked[:].rearrange("p (t g i) -> p g t i", i=PACK, t=PACK)
+        w_by_feature = quantize("w_by_feature", w_woven, E4M3, 2)
+        for half in range(2):
+            nc.vector.tensor_copy(woven_view[:, 64 * half : 64 * (half + 1)], picked_view[:, 64 * half : 64 * (half + 1)])
+        for half in range(2):
+            w_by_feature[2](half)
+
+        scaled = [tile("scaled%d" % j, K, F32) for j in range(PACK)]
+        probs = [tile("probs%d" % j, K, F32) for j in range(PACK)]
+        for j in range(PACK):
+            product(banks[4 + j], w_by_feature, j, E4M3, x_by_feature, E4M3)
+        for j in range(PACK):
+            nc.vector.tensor_tensor(scaled[j][:], banks[4 + j][:], us_free[:], MULT)
+            nc.scalar.activation(
+                out=probs[j][:], in_=scaled[j][:], func=SIGMOID, bias=kb_cols[:, j : j + 1], scale=ts_cols[:, j : j + 1]
+            )
+            for t in range(PACK):
+                turn(banks[j], t, probs[j][:, t * P : (t + 1) * P])
+
+        errs = [tile("errs%d" % j, K, F32) for j in range(PACK)]
+        h_rows = tile("h_rows", PACK * K, BF16)
+        h_by_row = quantize("h_by_row", h_rows, E5M2, PACK)
+        label_view = labels[:].rearrange("s (t j g i) -> s j g t i", t=PACK, j=PACK, i=PACK)
+
+        def err(j):
+            nc.vector.tensor_tensor(
+                errs[j][:].rearrange("s (g i t) -> s g t i", i=PACK, t=PACK),
+                banks[j][:].rearrange("s (t g i) -> s g t i", i=PACK, t=PACK),
+                label_view[:, j],
+                SUB,
+            )
+
+        def weigh(j):
+            cols = slice(j * K, (j + 1) * K)
+            nc.vector.tensor_tensor(h_rows[:, cols], errs[j][:], both_scales[:, cols], MULT)
+
+        err(0)
+        for j in range(1, PACK):
+            err(j)
+            weigh(j - 1)
+        h_by_row[2](0)
+        h_by_row[2](1)
+        weigh(PACK - 1)
+        h_by_row[2](2)
+        h_by_row[2](3)
+        w_by_slot = quantize("w_by_slot", w_turned, E4M3, 1)
+        w_by_slot[2](0)
+
+        out0_rows = out_0.rearrange("(p t) n -> p t n", t=PACK)
+        out1_rows = out_1.rearrange("(p t) n -> p t n", t=PACK)
+
+        def put(name, t, bank, stat, mov, window, offsets, rows):
+            product(bank, stat, t, E4M3, mov, E5M2)
+            sums = tile("%s%d" % (name, t), K, F32)
+            nc.scalar.copy(out=sums[:], in_=bank[:])
+            nc.vector.tensor_copy(window[:].indirect(offsets[:]), sums[:])
+            nc.sync.dma_start(out=rows[:, t, :], in_=window[:])
+
+        def put_tail(t):
+            put("dv", t, banks[4 + t], x_by_row, h_by_row, tail_windows[t % 2], tail_list, out0_rows)
+
+        put_tail(0)
+
+        h_slots = tile("h_slots", PACK * K, BF16)
+        h_words = h_rows[:].bitcast(F32)
+        slots_view = h_slots[:].rearrange("p (s u e t) -> p u s e t", u=2, e=2, t=PACK)
+        for u in range(2):
+            for t in range(PACK):
+                turn(banks[u], t, h_words[:, 2 * t + u : 2 * K : 2 * PACK])
+            nc.scalar.copy(
+                out=slots_view[:, u],
+                in_=banks[u][:].bitcast(BF16).rearrange("p (t s e) -> p s e t", t=PACK, e=2),
+            )
+        h_by_slot = quantize("h_by_slot", h_slots, E5M2, 1)
+        h_by_slot[2](0)
+
+        def put_head(t):
+            put("du", t, banks[(2 + t) % PACK], w_by_slot, h_by_slot, head_windows[t % 2], head_list, out1_rows)
+
+        put_tail(1)
+        put_head(0)
+        put_head(1)
+        put_tail(2)
+        put_tail(3)
+        put_head(2)
+        put_head(3)

@@ -12,12 +12,14 @@ E4M3 = mybir.dt.float8_e4m3fn_x4
 E5M2 = mybir.dt.float8_e5m2_x4
 MULT = mybir.AluOpType.mult
 SUB = mybir.AluOpType.subtract
+COPY = mybir.ActivationFunctionType.Copy
 SIGMOID = mybir.ActivationFunctionType.Sigmoid
 
 P = 128
 PACK = 4
 K = P * PACK
 TABLE = 2048
+ON_VECTOR = 2
 FLOPS = 3 * 2 * K * K * K
 
 
@@ -43,9 +45,9 @@ def tile_attend_gmf_nce_vu_kb_kernel(tc, uT, vT, y, us, ts, kb, offs, uoffs, out
 
         u_rows = uT.rearrange("(p t) n -> p t n", t=PACK)
         v_rows = vT.rearrange("(p t) n -> p t n", t=PACK)
-        nc.sync.dma_start(out=u_planes[0][:], in_=u_rows[:, 0, :])
-        nc.sync.dma_start(head_list[:], uoffs)
         nc.sync.dma_start(tail_list[:], offs)
+        nc.sync.dma_start(head_list[:], uoffs)
+        nc.sync.dma_start(out=u_planes[0][:], in_=u_rows[:, 0, :])
         nc.scalar.dma_start(out=ts_row[P - 1 : P, :], in_=ts[0:1, :])
         nc.scalar.dma_start(out=kb_row[P - 1 : P, :], in_=kb[0:1, :])
         nc.scalar.dma_start(out=us4[:], in_=us[0].rearrange("(s t) o -> s (t o)", t=PACK))
@@ -61,7 +63,7 @@ def tile_attend_gmf_nce_vu_kb_kernel(tc, uT, vT, y, us, ts, kb, offs, uoffs, out
         make_identity(nc, ident[:])
         warm = tile("warm", 1, F32)
         nc.scalar.activation(out=warm[:], in_=ident[:, 0:1], func=SIGMOID)
-        tail_windows = [tile("tail_window%d" % w, TABLE, F32) for w in range(2)]
+        tail_windows = [tile("tail_window%d" % w, TABLE, F32) for w in range(3)]
         head_windows = [tile("head_window%d" % w, TABLE, F32) for w in range(2)]
         for window in tail_windows + head_windows:
             nc.gpsimd.memset(window[:], 0.0)
@@ -108,6 +110,29 @@ def tile_attend_gmf_nce_vu_kb_kernel(tc, uT, vT, y, us, ts, kb, offs, uoffs, out
                 in_=bank[:, 0:256].rearrange("s (u p) -> s p u", u=2),
             )
 
+        ts_picked = tile("ts_picked", K, F32)
+        kb_picked = tile("kb_picked", K, F32)
+        ts_cols = tile("ts_cols", PACK, F32)
+        kb_cols = tile("kb_cols", PACK, F32)
+        for row, picked, cols, bank in ((ts_row, ts_picked, ts_cols, banks[0]), (kb_row, kb_picked, kb_cols, banks[1])):
+            nc.vector.tensor_copy(picked[:], row[:].indirect(tail_list[:]))
+            for j in range(PACK):
+                turn(bank, j, picked[:, j * P : (j + 1) * P])
+            nc.scalar.copy(out=cols[:], in_=bank[:, P - 1 : K : P])
+        for j in range(PACK):
+            turn(banks[2], j, ts_cols[:, j : j + 1].to_broadcast([P, P]))
+
+        scale_planes = tile("scale_planes", PACK * K, F32)
+        for t in range(PACK):
+            nc.scalar.activation(
+                out=scale_planes[:, t * K : (t + 1) * K], in_=banks[2][:], func=COPY, scale=us4[:, t : t + 1]
+            )
+        both_scales = tile("both_scales", PACK * K, F32)
+        nc.scalar.copy(
+            out=both_scales[:].rearrange("s (g i t) -> s g t i", i=PACK, t=PACK),
+            in_=scale_planes[:].rearrange("s (t g i) -> s g t i", i=PACK, t=PACK),
+        )
+
         x_picked = tile("x_picked", PACK * K, BF16)
         x_turned = tile("x_turned", PACK * K, BF16)
         gather_plane(x_picked, 0, u_planes[0], head_list)
@@ -121,29 +146,9 @@ def tile_attend_gmf_nce_vu_kb_kernel(tc, uT, vT, y, us, ts, kb, offs, uoffs, out
         gather_plane(x_picked, 1, u_planes[1], head_list)
         turn_plane(x_picked, 1, banks[5], x_turned)
 
-        ts_picked = tile("ts_picked", K, F32)
-        kb_picked = tile("kb_picked", K, F32)
-        ts_cols = tile("ts_cols", PACK, F32)
-        kb_cols = tile("kb_cols", PACK, F32)
-        for row, picked, cols, bank in ((ts_row, ts_picked, ts_cols, banks[0]), (kb_row, kb_picked, kb_cols, banks[1])):
-            nc.vector.tensor_copy(picked[:], row[:].indirect(tail_list[:]))
-            for j in range(PACK):
-                turn(bank, j, picked[:, j * P : (j + 1) * P])
-            nc.scalar.copy(out=cols[:], in_=bank[:, P - 1 : K : P])
-        for j in range(PACK):
-            turn(banks[2], j, ts_cols[:, j : j + 1].to_broadcast([P, P]))
-
         for t in range(2, PACK):
             gather_plane(x_picked, t, u_planes[t], head_list)
             turn_plane(x_picked, t, banks[4 + t], x_turned)
-
-        both_scales = tile("both_scales", PACK * K, F32)
-        nc.vector.tensor_tensor(
-            both_scales[:].rearrange("s (c t) -> s c t", t=PACK),
-            banks[2][:].unsqueeze(2).to_broadcast([P, K, PACK]),
-            us4[:].unsqueeze(1).to_broadcast([P, K, PACK]),
-            MULT,
-        )
 
         x_woven = tile("x_woven", PACK * K, BF16)
         nc.scalar.copy(
@@ -161,21 +166,28 @@ def tile_attend_gmf_nce_vu_kb_kernel(tc, uT, vT, y, us, ts, kb, offs, uoffs, out
         turn_plane(w_picked, 1, banks[1], w_turned)
         x_by_feature = quantize("x_by_feature", x_woven, E4M3, 1)
         x_by_feature[2](0)
-        for t in range(2, PACK):
-            gather_plane(w_picked, t, v_planes[t], tail_list)
-            turn_plane(w_picked, t, banks[t], w_turned)
+        gather_plane(w_picked, 2, v_planes[2], tail_list)
+        turn_plane(w_picked, 2, banks[2], w_turned)
+        for half in range(2):
+            nc.vector.tensor_copy(
+                w_picked[:, 3 * K + 256 * half : 3 * K + 256 * (half + 1)],
+                v_planes[3][:].indirect(tail_list[:, 16 * half : 16 * (half + 1)]),
+            )
 
         w_woven = tile("w_woven", PACK * K, BF16)
         woven_view = w_woven[:].rearrange("p (g i t) -> p g t i", i=PACK, t=PACK)
         picked_view = w_picked[:].rearrange("p (t g i) -> p g t i", i=PACK, t=PACK)
-        w_by_feature = quantize("w_by_feature", w_woven, E4M3, 2)
-        for half in range(2):
-            nc.vector.tensor_copy(woven_view[:, 64 * half : 64 * (half + 1)], picked_view[:, 64 * half : 64 * (half + 1)])
-        for half in range(2):
-            w_by_feature[2](half)
+        w_by_feature = quantize("w_by_feature", w_woven, E4M3, PACK)
+        for j in range(2):
+            nc.vector.tensor_copy(woven_view[:, 32 * j : 32 * (j + 1)], picked_view[:, 32 * j : 32 * (j + 1)])
+        for j in range(2, PACK):
+            nc.scalar.copy(out=woven_view[:, 32 * j : 32 * (j + 1)], in_=picked_view[:, 32 * j : 32 * (j + 1)])
+        for j in range(PACK):
+            w_by_feature[2](j)
 
         scaled = [tile("scaled%d" % j, K, F32) for j in range(PACK)]
         probs = [tile("probs%d" % j, K, F32) for j in range(PACK)]
+        minus_labels = {j: tile("minus_labels%d" % j, K, F32) for j in range(ON_VECTOR, PACK)}
         for j in range(PACK):
             product(banks[4 + j], w_by_feature, j, E4M3, x_by_feature, E4M3)
         for j in range(PACK):
@@ -183,10 +195,27 @@ def tile_attend_gmf_nce_vu_kb_kernel(tc, uT, vT, y, us, ts, kb, offs, uoffs, out
             nc.scalar.activation(
                 out=probs[j][:], in_=scaled[j][:], func=SIGMOID, bias=kb_cols[:, j : j + 1], scale=ts_cols[:, j : j + 1]
             )
-            for t in range(PACK):
-                turn(banks[j], t, probs[j][:, t * P : (t + 1) * P])
+            if j < ON_VECTOR:
+                for t in range(PACK):
+                    turn(banks[j], t, probs[j][:, t * P : (t + 1) * P])
+            if j == 0:
+                for n in range(ON_VECTOR, PACK):
+                    for t in range(PACK):
+                        turn(banks[n], t, labels[:, t * K + n * P : t * K + (n + 1) * P])
+                    nc.scalar.activation(out=minus_labels[n][:], in_=banks[n][:], func=COPY, scale=-1.0)
+            if j >= ON_VECTOR:
+                for n, src in enumerate((minus_labels[j], probs[j])):
+                    for t in range(PACK):
+                        nc.tensor.matmul(
+                            banks[j][:, t * P : (t + 1) * P],
+                            src[:, t * P : (t + 1) * P],
+                            ident[:],
+                            start=(n == 0 and t == 0),
+                            stop=(n == 1 and t == PACK - 1),
+                            is_transpose=True,
+                        )
 
-        errs = [tile("errs%d" % j, K, F32) for j in range(PACK)]
+        errs = [tile("errs%d" % j, K, F32) for j in range(ON_VECTOR)]
         h_rows = tile("h_rows", PACK * K, BF16)
         h_by_row = quantize("h_by_row", h_rows, E5M2, PACK)
         label_view = labels[:].rearrange("s (t j g i) -> s j g t i", t=PACK, j=PACK, i=PACK)
@@ -201,34 +230,47 @@ def tile_attend_gmf_nce_vu_kb_kernel(tc, uT, vT, y, us, ts, kb, offs, uoffs, out
 
         def weigh(j):
             cols = slice(j * K, (j + 1) * K)
-            nc.vector.tensor_tensor(h_rows[:, cols], errs[j][:], both_scales[:, cols], MULT)
+            if j < ON_VECTOR:
+                nc.vector.tensor_tensor(h_rows[:, cols], errs[j][:], both_scales[:, cols], MULT)
+            else:
+                nc.vector.tensor_tensor(
+                    h_rows[:, cols].rearrange("s (c t) -> s c t", t=PACK),
+                    banks[j][:].rearrange("s (t c) -> s c t", t=PACK),
+                    both_scales[:, cols].rearrange("s (c t) -> s c t", t=PACK),
+                    MULT,
+                )
 
-        err(0)
-        for j in range(1, PACK):
+        for j in range(ON_VECTOR):
             err(j)
-            weigh(j - 1)
+        weigh(0)
+        weigh(1)
+        weigh(2)
         h_by_row[2](0)
         h_by_row[2](1)
-        weigh(PACK - 1)
+        weigh(3)
         h_by_row[2](2)
         h_by_row[2](3)
+        turn_plane(w_picked, 3, banks[3], w_turned)
         w_by_slot = quantize("w_by_slot", w_turned, E4M3, 1)
         w_by_slot[2](0)
 
         out0_rows = out_0.rearrange("(p t) n -> p t n", t=PACK)
         out1_rows = out_1.rearrange("(p t) n -> p t n", t=PACK)
 
-        def put(name, t, bank, stat, mov, window, offsets, rows):
+        def put(sums, t, bank, stat, mov, window, offsets, rows, pieces):
             product(bank, stat, t, E4M3, mov, E5M2)
-            sums = tile("%s%d" % (name, t), K, F32)
-            nc.scalar.copy(out=sums[:], in_=bank[:])
-            nc.vector.tensor_copy(window[:].indirect(offsets[:]), sums[:])
+            width = K // pieces
+            for n in range(pieces):
+                cols = slice(n * width, (n + 1) * width)
+                nc.scalar.copy(out=sums[:, cols], in_=bank[:, cols])
+                nc.vector.tensor_copy(window[:].indirect(offsets[:, n * width // 16 : (n + 1) * width // 16]), sums[:, cols])
             nc.sync.dma_start(out=rows[:, t, :], in_=window[:])
 
         def put_tail(t):
-            put("dv", t, banks[4 + t], x_by_row, h_by_row, tail_windows[t % 2], tail_list, out0_rows)
+            put(scaled[t], t, banks[4 + t], x_by_row, h_by_row, tail_windows[t % 3], tail_list, out0_rows, 2 if t == 0 else 1)
 
         put_tail(0)
+        put_tail(1)
 
         h_slots = tile("h_slots", PACK * K, BF16)
         h_words = h_rows[:].bitcast(F32)
@@ -244,12 +286,11 @@ def tile_attend_gmf_nce_vu_kb_kernel(tc, uT, vT, y, us, ts, kb, offs, uoffs, out
         h_by_slot[2](0)
 
         def put_head(t):
-            put("du", t, banks[(2 + t) % PACK], w_by_slot, h_by_slot, head_windows[t % 2], head_list, out1_rows)
+            put(probs[t], t, banks[(2 + t) % PACK], w_by_slot, h_by_slot, head_windows[t % 2], head_list, out1_rows, 1)
 
-        put_tail(1)
+        put_tail(2)
         put_head(0)
         put_head(1)
-        put_tail(2)
         put_tail(3)
         put_head(2)
         put_head(3)

from contextlib import ExitStack

import concourse.mybir as mybir
from concourse.masks import make_identity

F32 = mybir.dt.float32
BF16 = mybir.dt.bfloat16
U32 = mybir.dt.uint32
U16 = mybir.dt.uint16
U8 = mybir.dt.uint8
E4M3 = mybir.dt.float8_e4m3fn_x4
E5M2 = mybir.dt.float8_e5m2_x4
MULT = mybir.AluOpType.mult
SUB = mybir.AluOpType.subtract
COPY = mybir.ActivationFunctionType.Copy
SIGMOID = mybir.ActivationFunctionType.Sigmoid

P = 128
PACK = 4
K = P * PACK
TABLE = 2048
ON_VECTOR = 2
FLOPS = 3 * 2 * K * K * K


def tile_attend_gmf_nce_vu_kb_kernel(tc, uT, vT, y, us, ts, kb, offs, uoffs, out_0, out_1):
    nc = tc.nc
    with ExitStack() as ctx:
        sb = ctx.enter_context(tc.tile_pool(name="sb", bufs=1))
        ps = ctx.enter_context(tc.psum_pool(name="ps", bufs=1))

        def tile(name, cols, dtype):
            return sb.tile([P, cols], dtype, name=name, align_bytes=64)

        banks = [ps.tile([P, K], F32, name="bank%d" % b) for b in range(8)]

        tail_list = tile("tail_list", K // 16, U16)
        head_list = tile("head_list", K // 16, U16)
        u_planes = [tile("u_plane%d" % t, TABLE, F32) for t in range(PACK)]
        v_planes = [tile("v_plane%d" % t, TABLE, F32) for t in range(PACK)]
        labels = tile("labels", PACK * K, F32)
        us4 = tile("us4", PACK, F32)
        ts_row = tile("ts_row", TABLE, F32)
        kb_row = tile("kb_row", TABLE, F32)

        u_rows = uT.rearrange("(p t) n -> p t n", t=PACK)
        v_rows = vT.rearrange("(p t) n -> p t n", t=PACK)
        nc.sync.dma_start(tail_list[:], offs)
        nc.sync.dma_start(head_list[:], uoffs)
        nc.sync.dma_start(out=u_planes[0][:], in_=u_rows[:, 0, :])
        nc.scalar.dma_start(out=ts_row[P - 1 : P, :], in_=ts[0:1, :])
        nc.scalar.dma_start(out=kb_row[P - 1 : P, :], in_=kb[0:1, :])
        nc.scalar.dma_start(out=us4[:], in_=us[0].rearrange("(s t) o -> s (t o)", t=PACK))
        nc.vector.memset(ts_row[0 : P - 1, :], 0.0)
        nc.vector.memset(kb_row[0 : P - 1, :], 0.0)
        for t in range(1, PACK):
            nc.sync.dma_start(out=u_planes[t][:], in_=u_rows[:, t, :])
        for t in range(PACK):
            nc.sync.dma_start(out=v_planes[t][:], in_=v_rows[:, t, :])
        nc.sync.dma_start(out=labels[:], in_=y[0].rearrange("(s t) i -> s (t i)", t=PACK))

        ident = tile("ident", P, F32)
        make_identity(nc, ident[:])
        warm = tile("warm", 1, F32)
        nc.scalar.activation(out=warm[:], in_=ident[:, 0:1], func=SIGMOID)
        tail_windows = [tile("tail_window%d" % w, TABLE, F32) for w in range(3)]
        head_windows = [tile("head_window%d" % w, TABLE, F32) for w in range(2)]
        for window in tail_windows + head_windows:
            nc.gpsimd.memset(window[:], 0.0)

        def turn(bank, block, src):
            nc.tensor.transpose(bank[:, block * P : (block + 1) * P], src, ident[:])

        def quantize(name, src, fmt, pieces):
            codes = tile(name + "_codes", K, U32)
            scales = tile(name + "_scales", K, U8)
            width = K // pieces

            def piece(n):
                cols = slice(n * width, (n + 1) * width)
                nc.vector.quantize_mx(
                    out=codes[:, cols].bitcast(fmt),
                    scales=scales[:, cols],
                    in_=src[:, PACK * n * width : PACK * (n + 1) * width],
                )

            return codes, scales, piece

        def product(bank, stat, block, stat_fmt, mov, mov_fmt):
            cols = slice(block * P, (block + 1) * P)
            nc.tensor.matmul_mx(
                out=bank[:],
                lhsT=stat[0][:, cols].bitcast(stat_fmt),
                lhsT_scale=stat[1][:, cols],
                rhs=mov[0][:].bitcast(mov_fmt),
                rhs_scale=mov[1][:],
                start=True,
                stop=True,
            )

        def gather_plane(picked, t, plane, offsets):
            nc.vector.tensor_copy(picked[:, t * K : (t + 1) * K], plane[:].indirect(offsets[:]))

        def turn_plane(picked, t, bank, turned):
            words = picked[:].bitcast(F32)
            for u in range(2):
                turn(bank, u, words[:, 256 * t + u : 256 * (t + 1) : 2])
            nc.scalar.copy(
                out=turned[:].bitcast(F32)[:, 256 * t : 256 * (t + 1)].rearrange("s (p u) -> s p u", u=2),
                in_=bank[:, 0:256].rearrange("s (u p) -> s p u", u=2),
            )

        ts_picked = tile("ts_picked", K, F32)
        kb_picked = tile("kb_picked", K, F32)
        ts_cols = tile("ts_cols", PACK, F32)
        kb_cols = tile("kb_cols", PACK, F32)
        for row, picked, cols, bank in ((ts_row, ts_picked, ts_cols, banks[0]), (kb_row, kb_picked, kb_cols, banks[1])):
            nc.vector.tensor_copy(picked[:], row[:].indirect(tail_list[:]))
            for j in range(PACK):
                turn(bank, j, picked[:, j * P : (j + 1) * P])
            nc.scalar.copy(out=cols[:], in_=bank[:, P - 1 : K : P])
        for j in range(PACK):
            turn(banks[2], j, ts_cols[:, j : j + 1].to_broadcast([P, P]))

        scale_planes = tile("scale_planes", PACK * K, F32)
        for t in range(PACK):
            nc.scalar.activation(
                out=scale_planes[:, t * K : (t + 1) * K], in_=banks[2][:], func=COPY, scale=us4[:, t : t + 1]
            )
        both_scales = tile("both_scales", PACK * K, F32)
        nc.scalar.copy(
            out=both_scales[:].rearrange("s (g i t) -> s g t i", i=PACK, t=PACK),
            in_=scale_planes[:].rearrange("s (t g i) -> s g t i", i=PACK, t=PACK),
        )

        x_picked = tile("x_picked", PACK * K, BF16)
        x_turned = tile("x_turned", PACK * K, BF16)
        gather_plane(x_picked, 0, u_planes[0], head_list)
        turn_plane(x_picked, 0, banks[4], x_turned)

        us_free = tile("us_free", K, F32)
        for t in range(PACK):
            turn(banks[3], t, us4[:, t : t + 1].to_broadcast([P, P]))
        nc.scalar.copy(out=us_free[:], in_=banks[3][:])

        gather_plane(x_picked, 1, u_planes[1], head_list)
        turn_plane(x_picked, 1, banks[5], x_turned)

        for t in range(2, PACK):
            gather_plane(x_picked, t, u_planes[t], head_list)
            turn_plane(x_picked, t, banks[4 + t], x_turned)

        x_woven = tile("x_woven", PACK * K, BF16)
        nc.scalar.copy(
            out=x_woven[:].rearrange("p (a s t) -> p s a t", a=PACK, t=PACK),
            in_=x_picked[:].rearrange("p (t s a) -> p s a t", a=PACK, t=PACK),
        )

        w_picked = tile("w_picked", PACK * K, BF16)
        w_turned = tile("w_turned", PACK * K, BF16)
        gather_plane(w_picked, 0, v_planes[0], tail_list)
        turn_plane(w_picked, 0, banks[0], w_turned)
        x_by_row = quantize("x_by_row", x_turned, E4M3, 1)
        x_by_row[2](0)
        gather_plane(w_picked, 1, v_planes[1], tail_list)
        turn_plane(w_picked, 1, banks[1], w_turned)
        x_by_feature = quantize("x_by_feature", x_woven, E4M3, 1)
        x_by_feature[2](0)
        gather_plane(w_picked, 2, v_planes[2], tail_list)
        turn_plane(w_picked, 2, banks[2], w_turned)
        for half in range(2):
            nc.vector.tensor_copy(
                w_picked[:, 3 * K + 256 * half : 3 * K + 256 * (half + 1)],
                v_planes[3][:].indirect(tail_list[:, 16 * half : 16 * (half + 1)]),
            )

        w_woven = tile("w_woven", PACK * K, BF16)
        woven_view = w_woven[:].rearrange("p (g i t) -> p g t i", i=PACK, t=PACK)
        picked_view = w_picked[:].rearrange("p (t g i) -> p g t i", i=PACK, t=PACK)
        w_by_feature = quantize("w_by_feature", w_woven, E4M3, PACK)
        for j in range(2):
            nc.vector.tensor_copy(woven_view[:, 32 * j : 32 * (j + 1)], picked_view[:, 32 * j : 32 * (j + 1)])
        for j in range(2, PACK):
            nc.scalar.copy(out=woven_view[:, 32 * j : 32 * (j + 1)], in_=picked_view[:, 32 * j : 32 * (j + 1)])
        for j in range(PACK):
            w_by_feature[2](j)

        scaled = [tile("scaled%d" % j, K, F32) for j in range(PACK)]
        probs = [tile("probs%d" % j, K, F32) for j in range(PACK)]
        minus_labels = {j: tile("minus_labels%d" % j, K, F32) for j in range(ON_VECTOR, PACK)}
        for j in range(PACK):
            product(banks[4 + j], w_by_feature, j, E4M3, x_by_feature, E4M3)
        for j in range(PACK):
            nc.vector.tensor_tensor(scaled[j][:], banks[4 + j][:], us_free[:], MULT)
            nc.scalar.activation(
                out=probs[j][:], in_=scaled[j][:], func=SIGMOID, bias=kb_cols[:, j : j + 1], scale=ts_cols[:, j : j + 1]
            )
            if j < ON_VECTOR:
                for t in range(PACK):
                    turn(banks[j], t, probs[j][:, t * P : (t + 1) * P])
            if j == 0:
                for n in range(ON_VECTOR, PACK):
                    for t in range(PACK):
                        turn(banks[n], t, labels[:, t * K + n * P : t * K + (n + 1) * P])
                    nc.scalar.activation(out=minus_labels[n][:], in_=banks[n][:], func=COPY, scale=-1.0)
            if j >= ON_VECTOR:
                for n, src in enumerate((minus_labels[j], probs[j])):
                    for t in range(PACK):
                        nc.tensor.matmul(
                            banks[j][:, t * P : (t + 1) * P],
                            src[:, t * P : (t + 1) * P],
                            ident[:],
                            start=(n == 0 and t == 0),
                            stop=(n == 1 and t == PACK - 1),
                            is_transpose=True,
                        )

        errs = [tile("errs%d" % j, K, F32) for j in range(ON_VECTOR)]
        h_rows = tile("h_rows", PACK * K, BF16)
        h_by_row = quantize("h_by_row", h_rows, E5M2, PACK)
        label_view = labels[:].rearrange("s (t j g i) -> s j g t i", t=PACK, j=PACK, i=PACK)

        def err(j):
            nc.vector.tensor_tensor(
                errs[j][:].rearrange("s (g i t) -> s g t i", i=PACK, t=PACK),
                banks[j][:].rearrange("s (t g i) -> s g t i", i=PACK, t=PACK),
                label_view[:, j],
                SUB,
            )

        def weigh(j):
            cols = slice(j * K, (j + 1) * K)
            if j < ON_VECTOR:
                nc.vector.tensor_tensor(h_rows[:, cols], errs[j][:], both_scales[:, cols], MULT)
            else:
                nc.vector.tensor_tensor(
                    h_rows[:, cols].rearrange("s (c t) -> s c t", t=PACK),
                    banks[j][:].rearrange("s (t c) -> s c t", t=PACK),
                    both_scales[:, cols].rearrange("s (c t) -> s c t", t=PACK),
                    MULT,
                )

        for j in range(ON_VECTOR):
            err(j)
        weigh(0)
        weigh(1)
        weigh(2)
        h_by_row[2](0)
        h_by_row[2](1)
        weigh(3)
        h_by_row[2](2)
        h_by_row[2](3)
        turn_plane(w_picked, 3, banks[3], w_turned)
        w_by_slot = quantize("w_by_slot", w_turned, E4M3, 1)
        w_by_slot[2](0)

        out0_rows = out_0.rearrange("(p t) n -> p t n", t=PACK)
        out1_rows = out_1.rearrange("(p t) n -> p t n", t=PACK)

        def put(sums, t, bank, stat, mov, window, offsets, rows, pieces):
            product(bank, stat, t, E4M3, mov, E5M2)
            width = K // pieces
            for n in range(pieces):
                cols = slice(n * width, (n + 1) * width)
                nc.scalar.copy(out=sums[:, cols], in_=bank[:, cols])
                nc.vector.tensor_copy(window[:].indirect(offsets[:, n * width // 16 : (n + 1) * width // 16]), sums[:, cols])
            nc.sync.dma_start(out=rows[:, t, :], in_=window[:])

        def put_tail(t):
            put(scaled[t], t, banks[4 + t], x_by_row, h_by_row, tail_windows[t % 3], tail_list, out0_rows, 2 if t == 0 else 1)

        put_tail(0)
        put_tail(1)

        h_slots = tile("h_slots", PACK * K, BF16)
        h_words = h_rows[:].bitcast(F32)
        slots_view = h_slots[:].rearrange("p (s u e t) -> p u s e t", u=2, e=2, t=PACK)
        for u in range(2):
            for t in range(PACK):
                turn(banks[u], t, h_words[:, 2 * t + u : 2 * K : 2 * PACK])
            nc.scalar.copy(
                out=slots_view[:, u],
                in_=banks[u][:].bitcast(BF16).rearrange("p (t s e) -> p s e t", t=PACK, e=2),
            )
        h_by_slot = quantize("h_by_slot", h_slots, E5M2, 1)
        h_by_slot[2](0)

        def put_head(t):
            put(probs[t], t, banks[(2 + t) % PACK], w_by_slot, h_by_slot, head_windows[t % 2], head_list, out1_rows, 1)

        put_tail(2)
        put_head(0)
        put_head(1)
        put_tail(3)
        put_head(2)
        put_head(3)
